import numpy as np
import ml_dtypes


def mxq(x, axis, fmt="e4m3"):
    dtype, down = {"e4m3": (ml_dtypes.float8_e4m3fn, 7), "e5m2": (ml_dtypes.float8_e5m2, 14)}[fmt]
    v = np.moveaxis(np.asarray(x, np.float32).astype(ml_dtypes.bfloat16).astype(np.float64), axis, -1)
    blocks = v.reshape(v.shape[:-1] + (-1, 32))
    amax = np.abs(blocks).max(-1, keepdims=True)
    byte = np.maximum(np.where(amax > 0, np.frexp(amax)[1] - 1 + 127, 0) - down, 1)
    scale = np.exp2(byte - 127.0)
    codes = (blocks / scale).astype(np.float32).astype(dtype).astype(np.float64)
    return np.moveaxis((codes * scale).reshape(v.shape), -1, axis)


WIDE = False


def mx_kscale(k):
    if not WIDE:
        return np.ones(k)
    levels = np.array([10, -10, 5, -5, 0])
    if k % 512:
        return np.exp2(np.random.permutation(np.resize(levels, k // 32))).repeat(32)
    a = np.empty((k // 512, 16))
    for p in range(k // 512):
        a[p, :8] = np.random.permutation(np.resize(levels, 8))
        for g in range(8):
            far = levels[np.abs(levels - a[p, g]) >= 10]
            a[p, g + 8] = far[np.random.randint(len(far))]
    return np.exp2(a.ravel()).repeat(32)


def f64(x):
    return np.asarray(x).astype(np.float64)


def striped(idx):
    return np.tile(idx.reshape(-1, 16).T, (8, 1)).astype(np.uint16)


def unstriped(offs):
    return offs[:16].T.reshape(-1).astype(np.int64)


E2M1 = np.array([0.0, 0.5, 1.0, 1.5, 2.0, 3.0, 4.0, 6.0, -0.0, -0.5, -1.0, -1.5, -2.0, -3.0, -4.0, -6.0])


def pack_weight(w, fmt):
    k, n = w.shape
    w = f64(np.asarray(w, np.float32).astype(ml_dtypes.bfloat16)).reshape(k // 32, 32, n)
    amax = np.abs(w).max(1)
    if fmt == "e4m3":
        byte = np.frexp(amax)[1] - 1 + 127 - 7
    else:
        mant, ex = np.frexp(amax / 6.0)
        byte = np.where(mant > 0.5, ex, ex - 1) + 127
    byte = np.clip(np.where(amax > 0, byte, 1), 1, 254)
    scaled = (w * np.exp2(127.0 - byte)[:, None, :]).reshape(k, n).astype(np.float32)
    by_word = np.ascontiguousarray(scaled.reshape(k // 512, 128, 4, n).transpose(0, 1, 3, 2))
    if fmt == "e4m3":
        words = by_word.astype(ml_dtypes.float8_e4m3fn).view(np.uint8)
    else:
        c = by_word.astype(ml_dtypes.float4_e2m1fn).view(np.uint8) & 0xF
        words = (c[..., 0::2] | (c[..., 1::2] << 4)).reshape(k // 512, 128, 2 * n)
    return np.ascontiguousarray(words), np.ascontiguousarray(byte.astype(np.uint8).reshape(k // 512, 16, n))


def unpack_weight(words, scales, fmt):
    g, _, n = scales.shape
    words = np.ascontiguousarray(words).reshape(g, 128, n, -1)
    if fmt == "e4m3":
        vals = words.view(ml_dtypes.float8_e4m3fn).astype(np.float64)
    else:
        nib = np.empty((g, 128, n, 4), np.uint8)
        nib[..., 0::2] = words & 0xF
        nib[..., 1::2] = words >> 4
        vals = E2M1[nib]
    vals = vals * np.repeat(np.exp2(scales.astype(np.float64) - 127.0), 8, axis=1)[..., None]
    return vals.transpose(0, 1, 3, 2).reshape(g * 512, n)


def pack_table(v):
    words, scales = pack_weight(v, "e4m3")
    return np.concatenate([words.reshape(words.shape[0], -1), scales.reshape(scales.shape[0], -1)], axis=1)


def unpack_table(tab):
    g, t = tab.shape[0], tab.shape[1] // 528
    return unpack_weight(tab[:, :512 * t].reshape(g, 128, t, 4), tab[:, 512 * t:].reshape(g, 16, t), "e4m3")


K, H, M, T, S = 1024, 1536, 512, 512, 256


def setup_inputs():
    n = np.random.standard_normal
    s = mx_kscale(K)[:, None]
    u = mx_kscale(H)[:, None]
    w2 = 1.4 * n((H, M)) / np.sqrt(H) / u
    p_w8 = pack_weight(w2[:512], "e4m3")
    p_w4 = pack_weight(w2[512:], "e2m1")
    return {
        "tab": pack_table(n((K, T)) * s),
        "w1": (n((K, H)) / np.sqrt(K) / s * u.T).astype(np.float32),
        "w8_words": p_w8[0],
        "w8_scales": p_w8[1],
        "w4_words": p_w4[0],
        "w4_scales": p_w4[1],
        "prev": (n((512, 256))).astype(np.float32),
        "offs": striped(np.random.permutation(T)[:S]),
    }


def reference(tab, w1, w8_words, w8_scales, w4_words, w4_scales, prev, offs):
    tab_ = unpack_table(tab)[:, unstriped(offs)]
    w1_ = mxq(f64(w1), 0, "e4m3")
    w8_ = unpack_weight(w8_words, w8_scales, "e4m3")
    w4_ = unpack_weight(w4_words, w4_scales, "e2m1")
    h_ = mxq(np.maximum(w1_.T @ tab_, 0.0), 0, "e4m3")
    y = w8_.T @ h_[:512] + w4_.T @ h_[512:]
    return f64(prev) + y

@@ -1,0 +1,197 @@
+from contextlib import ExitStack
+
+import concourse.mybir as mybir
+
+FLOPS = 1207959552
+
+P = 128
+K, H, M, T, S = 1024, 1536, 512, 512, 256
+HALF = 128
+WORD_BYTES = 512 * T
+
+F32 = mybir.dt.float32
+BF16 = mybir.dt.bfloat16
+I32 = mybir.dt.int32
+U32 = mybir.dt.uint32
+U16 = mybir.dt.uint16
+U8 = mybir.dt.uint8
+FP8 = mybir.dt.float8_e4m3fn_x4
+FP4 = mybir.dt.float4_e2m1fn_x4
+RELU = mybir.ActivationFunctionType.Relu
+
+
+def tile_list_tabmlp_mix_res_kernel(
+    tc, tab, w1, w8_words, w8_scales, w4_words, w4_scales, prev, offs, out
+):
+    nc = tc.nc
+    with ExitStack() as ctx:
+        keep = ctx.enter_context(tc.tile_pool(name="keep", bufs=1))
+        psum = ctx.enter_context(tc.psum_pool(name="psum", bufs=1))
+
+        offsets = keep.tile([P, S // 16], U16, name="offsets")
+        table_words = [keep.tile([P, T], I32, name=f"table_words{a}", align_bytes=64) for a in range(2)]
+        table_scales = keep.tile([P, T // 4], I32, name="table_scales", align_bytes=64)
+        w2_scales = keep.tile([P, 3, M // 4], I32, name="w2_scales", align_bytes=64)
+        w8_codes = keep.tile([P, M], I32, name="w8_codes", align_bytes=64)
+        w4_codes = keep.tile([P, 2, M // 2], I32, name="w4_codes", align_bytes=64)
+        prev_sb = keep.tile([P, 4, S], F32, name="prev_sb")
+
+        nc.vector.memset(table_scales[:], 0)
+        nc.vector.memset(w2_scales[:], 0)
+
+        def load_w1(a, b, c0, c1):
+            raw = keep.tile([P, 4, c1 - c0], F32, name=f"raw{a}{b}_{c0}")
+            rows = w1[512 * a : 512 * (a + 1), 512 * b + c0 : 512 * b + c1]
+            nc.sync.dma_start(raw[:], rows.rearrange("(p j) c -> p j c", j=4))
+            return raw
+
+        tab_i32 = tab.bitcast(I32)
+        tab_scale_rows = tab_i32[:, WORD_BYTES // 4 :].rearrange("a (q c) -> a q c", q=16)
+        w8_rows = w8_scales.bitcast(I32)
+        w4_rows = w4_scales.bitcast(I32)
+
+        def load_w8_scales(q):
+            nc.sync.dma_start(w2_scales[32 * q : 32 * q + 4, 0, :], w8_rows[0, 4 * q : 4 * q + 4, :])
+
+        def load_w4_scales(q):
+            nc.sync.dma_start(
+                w2_scales[32 * q : 32 * q + 4, 1:3, :], w4_rows[:, 4 * q : 4 * q + 4, :].rearrange("a q c -> q a c")
+            )
+
+        raws = {}
+        for a in range(2):
+            nc.sync.dma_start(
+                table_words[a][:], tab_i32[a, 0 : WORD_BYTES // 4].rearrange("(p c) -> p c", p=P)
+            )
+        nc.sync.dma_start(offsets[:], offs)
+        raws[0, 0] = [(0, 512, load_w1(0, 0, 0, 512))]
+        for q in range(4):
+            nc.sync.dma_start(table_scales[32 * q : 32 * q + 8, :], tab_scale_rows[:, 4 * q : 4 * q + 4, :])
+        raws[0, 1] = [(0, 512, load_w1(1, 0, 0, 512))]
+        load_w8_scales(0)
+        load_w8_scales(1)
+        raws[1, 0] = [(0, 512, load_w1(0, 1, 0, 512))]
+        load_w8_scales(2)
+        load_w8_scales(3)
+        load_w4_scales(0)
+        load_w4_scales(1)
+        raws[1, 1] = [(0, 512, load_w1(1, 1, 0, 512))]
+        load_w4_scales(2)
+        load_w4_scales(3)
+        raws[2, 0] = [(0, 512, load_w1(0, 2, 0, 512))]
+        raws[2, 1] = [(c0, c1, load_w1(1, 2, c0, c1)) for c0, c1 in ((0, 256), (256, 384), (384, 512))]
+        nc.sync.dma_start(w8_codes[:], w8_words[0].rearrange("p n i -> p (n i)").bitcast(I32))
+        nc.sync.dma_start(w4_codes[:], w4_words.bitcast(I32).rearrange("a p c -> p a c"))
+        nc.sync.dma_start(prev_sb[:], prev.rearrange("(m p) j -> p m j", p=P))
+
+        picked_words = []
+        for a in range(2):
+            words = keep.tile([P, S], U32, name=f"picked_words{a}", align_bytes=64)
+            nc.vector.tensor_copy(words[:], table_words[a][:].bitcast(U32).indirect(offsets[:]))
+            picked_words.append(words)
+        picked_scales = keep.tile([P, S], U8, name="picked_scales", align_bytes=64)
+        nc.vector.tensor_copy(picked_scales[:], table_scales[:].bitcast(U8).indirect(offsets[:]))
+
+        codes, scales = {}, {}
+
+        def prepare(b, a):
+            last = (b, a) == (2, 1)
+            pair = []
+            for e in range(2):
+                grouped = keep.tile([P, 1024], BF16, name=f"grouped{b}{a}{e}", align_bytes=64)
+                pair.append(grouped)
+            for c0, c1, raw in raws[b, a]:
+                src = raw[:].rearrange("p j (m t) -> p m j t", t=4)
+                for e, copy in ((1, nc.scalar.copy), (0, nc.vector.tensor_copy)):
+                    view = pair[e][:].rearrange("p (t m j) -> p m j t", t=2, j=4)
+                    copy(view[:, c0 // 4 : c1 // 4], src[:, :, :, 2 * e : 2 * e + 2])
+            w = keep.tile([P, 512], U32, name=f"w1_codes{b}{a}", align_bytes=64)
+            s = keep.tile([P, 512], U8, name=f"w1_scales{b}{a}", align_bytes=64)
+            step = 512 if last else 1024
+            for i in range(0, 2048, step):
+                o = slice(i // 4, (i + step) // 4)
+                e, r = divmod(i, 1024)
+                nc.vector.quantize_mx(out=w[:, o].bitcast(FP8), scales=s[:, o], in_=pair[e][:, r : r + step])
+            codes[b, a] = w
+            scales[b, a] = s
+
+        def hidden_matmuls(b):
+            banks = [psum.tile([P, 4, HALF], F32, name=f"hidden{h}") for h in range(2)]
+            for t in range(4):
+                cols = slice(HALF * t, HALF * (t + 1))
+                for a in range(2):
+                    for h in range(2):
+                        toks = slice(HALF * h, HALF * (h + 1))
+                        nc.tensor.matmul_mx(
+                            out=banks[h][:, t, :],
+                            lhsT=codes[b, a][:, cols].bitcast(FP8),
+                            lhsT_scale=scales[b, a][:, cols],
+                            rhs=picked_words[a][:, toks].bitcast(FP8),
+                            rhs_scale=picked_scales[4 * a : P, toks],
+                            start=a == 0,
+                            stop=a == 1,
+                        )
+            return banks
+
+        h_codes, h_scales = {}, {}
+
+        def hidden_quantise(b, banks):
+            grouped = [keep.tile([P, HALF, 4], BF16, name=f"h_grouped{b}{h}", align_bytes=64) for h in range(2)]
+            nc.scalar.activation(grouped[0][:], banks[0][:].rearrange("p t n -> p n t"), RELU)
+            nc.vector.tensor_scalar_max(grouped[1][:], banks[1][:].rearrange("p t n -> p n t"), 0.0)
+            for h in range(2):
+                w = keep.tile([P, HALF], U32, name=f"h_codes{b}{h}", align_bytes=64)
+                s = keep.tile([P, HALF], U8, name=f"h_scales{b}{h}", align_bytes=64)
+                nc.vector.quantize_mx(
+                    out=w[:].bitcast(FP8), scales=s[:], in_=grouped[h][:].rearrange("p n t -> p (n t)")
+                )
+                h_codes[b, h] = w
+                h_scales[b, h] = s
+
+        def out_matmul(acc, m, h, b):
+            if b == 0:
+                lhsT = w8_codes[:, HALF * m : HALF * (m + 1)].bitcast(FP8)
+            else:
+                lhsT = w4_codes[:, b - 1, 64 * m : 64 * (m + 1)].bitcast(FP4)
+            nc.tensor.matmul_mx(
+                out=acc[:],
+                lhsT=lhsT,
+                lhsT_scale=w2_scales[:, b, 32 * m : 32 * (m + 1)].bitcast(U8),
+                rhs=h_codes[b, h][:].bitcast(FP8),
+                rhs_scale=h_scales[b, h][:],
+                start=b == 0,
+                stop=b == 2,
+            )
+
+        prepare(0, 0)
+        prepare(0, 1)
+        banks = hidden_matmuls(0)
+        prepare(1, 0)
+        hidden_quantise(0, banks)
+        prepare(1, 1)
+        banks = hidden_matmuls(1)
+        prepare(2, 0)
+        hidden_quantise(1, banks)
+        prepare(2, 1)
+
+        groups = [(m, h) for m in range(4) for h in range(2)]
+        acc = {}
+        for m, h in groups[:6]:
+            acc[m, h] = psum.tile([P, HALF], F32, name=f"acc{m}{h}")
+            out_matmul(acc[m, h], m, h, 0)
+        banks = hidden_matmuls(2)
+        for m, h in groups[:6]:
+            out_matmul(acc[m, h], m, h, 1)
+        hidden_quantise(2, banks)
+        for m, h in groups[6:]:
+            acc[m, h] = psum.tile([P, HALF], F32, name=f"hidden{h}")
+            out_matmul(acc[m, h], m, h, 0)
+            out_matmul(acc[m, h], m, h, 1)
+        for m in range(4):
+            res = keep.tile([P, S], F32, name=f"res{m}")
+            for h in range(2):
+                out_matmul(acc[m, h], m, h, 2)
+                toks = slice(HALF * h, HALF * (h + 1))
+                nc.vector.tensor_add(res[:, toks], acc[m, h][:], prev_sb[:, m, toks])
+            queue = nc.sync if m % 2 == 0 else nc.scalar
+            queue.dma_start(out[P * m : P * (m + 1), :], res[:])

@@ -39,11 +39,13 @@ def tile_list_tabmlp_mix_res_kernel(
         nc.vector.memset(table_scales[:], 0)
         nc.vector.memset(w2_scales[:], 0)
 
+        raws = {}
+
         def load_w1(a, b, c0, c1):
-            raw = keep.tile([P, 4, c1 - c0], F32, name=f"raw{a}{b}_{c0}")
+            raw = keep.tile([P, 4, c1 - c0], F32, name=f"raw{a}{b}_{c0}", align_bytes=64)
             rows = w1[512 * a : 512 * (a + 1), 512 * b + c0 : 512 * b + c1]
             nc.sync.dma_start(raw[:], rows.rearrange("(p j) c -> p j c", j=4))
-            return raw
+            raws.setdefault((b, a), []).append((c0, c1, raw))
 
         tab_i32 = tab.bitcast(I32)
         tab_scale_rows = tab_i32[:, WORD_BYTES // 4 :].rearrange("a (q c) -> a q c", q=16)
@@ -58,28 +60,28 @@ def tile_list_tabmlp_mix_res_kernel(
                 w2_scales[32 * q : 32 * q + 4, 1:3, :], w4_rows[:, 4 * q : 4 * q + 4, :].rearrange("a q c -> q a c")
             )
 
-        raws = {}
         for a in range(2):
             nc.sync.dma_start(
                 table_words[a][:], tab_i32[a, 0 : WORD_BYTES // 4].rearrange("(p c) -> p c", p=P)
             )
         nc.sync.dma_start(offsets[:], offs)
-        raws[0, 0] = [(0, 512, load_w1(0, 0, 0, 512))]
+        load_w1(0, 0, 0, 512)
         for q in range(4):
             nc.sync.dma_start(table_scales[32 * q : 32 * q + 8, :], tab_scale_rows[:, 4 * q : 4 * q + 4, :])
-        raws[0, 1] = [(0, 512, load_w1(1, 0, 0, 512))]
+        load_w1(1, 0, 0, 512)
         load_w8_scales(0)
         load_w8_scales(1)
-        raws[1, 0] = [(0, 512, load_w1(0, 1, 0, 512))]
+        load_w1(0, 1, 0, 512)
         load_w8_scales(2)
         load_w8_scales(3)
         load_w4_scales(0)
         load_w4_scales(1)
-        raws[1, 1] = [(0, 512, load_w1(1, 1, 0, 512))]
+        load_w1(1, 1, 0, 512)
         load_w4_scales(2)
         load_w4_scales(3)
-        raws[2, 0] = [(0, 512, load_w1(0, 2, 0, 512))]
-        raws[2, 1] = [(c0, c1, load_w1(1, 2, c0, c1)) for c0, c1 in ((0, 256), (256, 384), (384, 512))]
+        load_w1(0, 2, 0, 512)
+        for c0, c1 in ((0, 256), (256, 384), (384, 512)):
+            load_w1(1, 2, c0, c1)
         nc.sync.dma_start(w8_codes[:], w8_words[0].rearrange("p n i -> p (n i)").bitcast(I32))
         nc.sync.dma_start(w4_codes[:], w4_words.bitcast(I32).rearrange("a p c -> p a c"))
         nc.sync.dma_start(prev_sb[:], prev.rearrange("(m p) j -> p m j", p=P))
@@ -92,31 +94,33 @@ def tile_list_tabmlp_mix_res_kernel(
         picked_scales = keep.tile([P, S], U8, name="picked_scales", align_bytes=64)
         nc.vector.tensor_copy(picked_scales[:], table_scales[:].bitcast(U8).indirect(offsets[:]))
 
-        codes, scales = {}, {}
+        grouped, codes, scales = {}, {}, {}
+        for b in range(3):
+            for a in range(2):
+                for e in range(2):
+                    grouped[b, a, e] = keep.tile([P, 1024], BF16, name=f"grouped{b}{a}{e}", align_bytes=64)
+                codes[b, a] = keep.tile([P, 512], U32, name=f"w1_codes{b}{a}", align_bytes=64)
+                scales[b, a] = keep.tile([P, 512], U8, name=f"w1_scales{b}{a}", align_bytes=64)
 
-        def prepare(b, a):
-            last = (b, a) == (2, 1)
-            pair = []
-            for e in range(2):
-                grouped = keep.tile([P, 1024], BF16, name=f"grouped{b}{a}{e}", align_bytes=64)
-                pair.append(grouped)
+        def interleave(b, a):
             for c0, c1, raw in raws[b, a]:
                 src = raw[:].rearrange("p j (m t) -> p m j t", t=4)
                 for e, copy in ((1, nc.scalar.copy), (0, nc.vector.tensor_copy)):
-                    view = pair[e][:].rearrange("p (t m j) -> p m j t", t=2, j=4)
+                    view = grouped[b, a, e][:].rearrange("p (t m j) -> p m j t", t=2, j=4)
                     copy(view[:, c0 // 4 : c1 // 4], src[:, :, :, 2 * e : 2 * e + 2])
-            w = keep.tile([P, 512], U32, name=f"w1_codes{b}{a}", align_bytes=64)
-            s = keep.tile([P, 512], U8, name=f"w1_scales{b}{a}", align_bytes=64)
-            step = 512 if last else 1024
+
+        def quantise(b, a, step):
             for i in range(0, 2048, step):
                 o = slice(i // 4, (i + step) // 4)
                 e, r = divmod(i, 1024)
-                nc.vector.quantize_mx(out=w[:, o].bitcast(FP8), scales=s[:, o], in_=pair[e][:, r : r + step])
-            codes[b, a] = w
-            scales[b, a] = s
+                nc.vector.quantize_mx(
+                    out=codes[b, a][:, o].bitcast(FP8),
+                    scales=scales[b, a][:, o],
+                    in_=grouped[b, a, e][:, r : r + step],
+                )
 
         def hidden_matmuls(b):
-            banks = [psum.tile([P, 4, HALF], F32, name=f"hidden{h}") for h in range(2)]
+            banks = [psum.tile([P, 4, HALF], F32, name=f"hidden{b % 2}{h}") for h in range(2)]
             for t in range(4):
                 cols = slice(HALF * t, HALF * (t + 1))
                 for a in range(2):
@@ -133,20 +137,30 @@ def tile_list_tabmlp_mix_res_kernel(
                         )
             return banks
 
-        h_codes, h_scales = {}, {}
+        h_grouped, h_codes, h_scales = {}, {}, {}
+        shared = {(1, 0): "raw12_384", (1, 1): "grouped211"}
+        for b in range(3):
+            h_codes[b] = keep.tile([P, S], U32, name=f"h_codes{b}", align_bytes=64)
+            h_scales[b] = keep.tile([P, S], U8, name=f"h_scales{b}", align_bytes=64)
 
-        def hidden_quantise(b, banks):
-            grouped = [keep.tile([P, HALF, 4], BF16, name=f"h_grouped{b}{h}", align_bytes=64) for h in range(2)]
-            nc.scalar.activation(grouped[0][:], banks[0][:].rearrange("p t n -> p n t"), RELU)
-            nc.vector.tensor_scalar_max(grouped[1][:], banks[1][:].rearrange("p t n -> p n t"), 0.0)
+        def relu(engine, b, h, bank):
+            name = shared.get((b, h), f"h_grouped{b}{h}")
+            tile = keep.tile([P, HALF, 4], BF16, name=name, align_bytes=64)
+            src = bank[:].rearrange("p t n -> p n t")
+            if engine is nc.scalar:
+                nc.scalar.activation(tile[:], src, RELU)
+            else:
+                nc.vector.tensor_scalar_max(tile[:], src, 0.0)
+            h_grouped[b, h] = tile
+
+        def hidden_quantise(b):
             for h in range(2):
-                w = keep.tile([P, HALF], U32, name=f"h_codes{b}{h}", align_bytes=64)
-                s = keep.tile([P, HALF], U8, name=f"h_scales{b}{h}", align_bytes=64)
+                toks = slice(HALF * h, HALF * (h + 1))
                 nc.vector.quantize_mx(
-                    out=w[:].bitcast(FP8), scales=s[:], in_=grouped[h][:].rearrange("p n t -> p (n t)")
+                    out=h_codes[b][:, toks].bitcast(FP8),
+                    scales=h_scales[b][:, toks],
+                    in_=h_grouped[b, h][:].rearrange("p n t -> p (n t)"),
                 )
-                h_codes[b, h] = w
-                h_scales[b, h] = s
 
         def out_matmul(acc, m, h, b):
             if b == 0:
@@ -157,37 +171,19 @@ def tile_list_tabmlp_mix_res_kernel(
                 out=acc[:],
                 lhsT=lhsT,
                 lhsT_scale=w2_scales[:, b, 32 * m : 32 * (m + 1)].bitcast(U8),
-                rhs=h_codes[b, h][:].bitcast(FP8),
-                rhs_scale=h_scales[b, h][:],
+                rhs=h_codes[b][:, HALF * h : HALF * (h + 1)].bitcast(FP8),
+                rhs_scale=h_scales[b][:, HALF * h : HALF * (h + 1)],
                 start=b == 0,
                 stop=b == 2,
             )
 
-        prepare(0, 0)
-        prepare(0, 1)
-        banks = hidden_matmuls(0)
-        prepare(1, 0)
-        hidden_quantise(0, banks)
-        prepare(1, 1)
-        banks = hidden_matmuls(1)
-        prepare(2, 0)
-        hidden_quantise(1, banks)
-        prepare(2, 1)
-
-        groups = [(m, h) for m in range(4) for h in range(2)]
         acc = {}
-        for m, h in groups[:6]:
-            acc[m, h] = psum.tile([P, HALF], F32, name=f"acc{m}{h}")
+
+        def start_out(m, h, name):
+            acc[m, h] = psum.tile([P, HALF], F32, name=name)
             out_matmul(acc[m, h], m, h, 0)
-        banks = hidden_matmuls(2)
-        for m, h in groups[:6]:
-            out_matmul(acc[m, h], m, h, 1)
-        hidden_quantise(2, banks)
-        for m, h in groups[6:]:
-            acc[m, h] = psum.tile([P, HALF], F32, name=f"hidden{h}")
-            out_matmul(acc[m, h], m, h, 0)
-            out_matmul(acc[m, h], m, h, 1)
-        for m in range(4):
+
+        def finish_out(m):
             res = keep.tile([P, S], F32, name=f"res{m}")
             for h in range(2):
                 out_matmul(acc[m, h], m, h, 2)
@@ -195,3 +191,42 @@ def tile_list_tabmlp_mix_res_kernel(
                 nc.vector.tensor_add(res[:, toks], acc[m, h][:], prev_sb[:, m, toks])
             queue = nc.sync if m % 2 == 0 else nc.scalar
             queue.dma_start(out[P * m : P * (m + 1), :], res[:])
+
+        interleave(0, 0)
+        quantise(0, 0, 1024)
+        interleave(0, 1)
+        quantise(0, 1, 1024)
+        banks = hidden_matmuls(0)
+        interleave(1, 0)
+        quantise(1, 0, 1024)
+        interleave(1, 1)
+        relu(nc.scalar, 0, 0, banks[0])
+        relu(nc.vector, 0, 1, banks[1])
+        quantise(1, 1, 1024)
+        banks = hidden_matmuls(1)
+        hidden_quantise(0)
+        interleave(2, 0)
+        quantise(2, 0, 1024)
+        interleave(2, 1)
+        quantise(2, 1, 512)
+        relu(nc.scalar, 1, 0, banks[0])
+        relu(nc.vector, 1, 1, banks[1])
+        hidden_quantise(1)
+        banks = hidden_matmuls(2)
+        for m in range(2):
+            for h in range(2):
+                start_out(m, h, f"acc{m}{h}")
+        for h in range(2):
+            start_out(2, h, f"hidden1{h}")
+        for m in range(3):
+            for h in range(2):
+                out_matmul(acc[m, h], m, h, 1)
+        relu(nc.scalar, 2, 0, banks[0])
+        relu(nc.vector, 2, 1, banks[1])
+        hidden_quantise(2)
+        for m in range(3):
+            finish_out(m)
+        for h in range(2):
+            start_out(3, h, f"hidden0{h}")
+            out_matmul(acc[3, h], 3, h, 1)
+        finish_out(3)

@@ -53,10 +53,10 @@ def tile_list_tabmlp_mix_res_kernel(
         w4_rows = w4_scales.bitcast(I32)
 
         def load_w8_scales(q):
-            nc.sync.dma_start(w2_scales[32 * q : 32 * q + 4, 0, :], w8_rows[0, 4 * q : 4 * q + 4, :])
+            nc.gpsimd.dma_start(w2_scales[32 * q : 32 * q + 4, 0, :], w8_rows[0, 4 * q : 4 * q + 4, :])
 
         def load_w4_scales(q):
-            nc.sync.dma_start(
+            nc.gpsimd.dma_start(
                 w2_scales[32 * q : 32 * q + 4, 1:3, :], w4_rows[:, 4 * q : 4 * q + 4, :].rearrange("a q c -> q a c")
             )
 
@@ -68,20 +68,16 @@ def tile_list_tabmlp_mix_res_kernel(
         load_w1(0, 0, 0, 512)
         for q in range(4):
             nc.sync.dma_start(table_scales[32 * q : 32 * q + 8, :], tab_scale_rows[:, 4 * q : 4 * q + 4, :])
+        for q in range(4):
+            load_w8_scales(q)
+        for q in range(4):
+            load_w4_scales(q)
         load_w1(1, 0, 0, 512)
-        load_w8_scales(0)
-        load_w8_scales(1)
         load_w1(0, 1, 0, 512)
-        load_w8_scales(2)
-        load_w8_scales(3)
-        load_w4_scales(0)
-        load_w4_scales(1)
         load_w1(1, 1, 0, 512)
-        load_w4_scales(2)
-        load_w4_scales(3)
         load_w1(0, 2, 0, 512)
-        for c0, c1 in ((0, 256), (256, 384), (384, 512)):
-            load_w1(1, 2, c0, c1)
+        load_w1(1, 2, 0, 384)
+        load_w1(1, 2, 384, 512)
         nc.sync.dma_start(w8_codes[:], w8_words[0].rearrange("p n i -> p (n i)").bitcast(I32))
         nc.sync.dma_start(w4_codes[:], w4_words.bitcast(I32).rearrange("a p c -> p a c"))
         nc.sync.dma_start(prev_sb[:], prev.rearrange("(m p) j -> p m j", p=P))
@@ -105,7 +101,8 @@ def tile_list_tabmlp_mix_res_kernel(
         def interleave(b, a):
             for c0, c1, raw in raws[b, a]:
                 src = raw[:].rearrange("p j (m t) -> p m j t", t=4)
-                for e, copy in ((1, nc.scalar.copy), (0, nc.vector.tensor_copy)):
+                for e in (1, 0):
+                    copy = nc.scalar.copy if e == 1 and c0 == 0 else nc.vector.tensor_copy
                     view = grouped[b, a, e][:].rearrange("p (t m j) -> p m j t", t=2, j=4)
                     copy(view[:, c0 // 4 : c1 // 4], src[:, :, :, 2 * e : 2 * e + 2])
 
@@ -189,8 +186,12 @@ def tile_list_tabmlp_mix_res_kernel(
                 out_matmul(acc[m, h], m, h, 2)
                 toks = slice(HALF * h, HALF * (h + 1))
                 nc.vector.tensor_add(res[:, toks], acc[m, h][:], prev_sb[:, m, toks])
-            queue = nc.sync if m % 2 == 0 else nc.scalar
-            queue.dma_start(out[P * m : P * (m + 1), :], res[:])
+                if m == 3:
+                    queue = nc.scalar if h == 0 else nc.sync
+                    queue.dma_start(out[P * m : P * (m + 1), toks], res[:, toks])
+            if m < 3:
+                queue = nc.scalar if m == 1 else nc.sync
+                queue.dma_start(out[P * m : P * (m + 1), :], res[:])
 
         interleave(0, 0)
         quantise(0, 0, 1024)
@@ -223,10 +224,9 @@ def tile_list_tabmlp_mix_res_kernel(
                 out_matmul(acc[m, h], m, h, 1)
         relu(nc.scalar, 2, 0, banks[0])
         relu(nc.vector, 2, 1, banks[1])
-        hidden_quantise(2)
-        for m in range(3):
-            finish_out(m)
         for h in range(2):
             start_out(3, h, f"hidden0{h}")
             out_matmul(acc[3, h], 3, h, 1)
-        finish_out(3)
+        hidden_quantise(2)
+        for m in range(4):
+            finish_out(m)

@@ -93,27 +93,27 @@ def tile_list_tabmlp_mix_res_kernel(
         grouped, codes, scales = {}, {}, {}
         for b in range(3):
             for a in range(2):
-                for e in range(2):
-                    grouped[b, a, e] = keep.tile([P, 1024], BF16, name=f"grouped{b}{a}{e}", align_bytes=64)
+                grouped[b, a] = keep.tile([P, 2048], BF16, name=f"grouped{b}{a}", align_bytes=64)
                 codes[b, a] = keep.tile([P, 512], U32, name=f"w1_codes{b}{a}", align_bytes=64)
                 scales[b, a] = keep.tile([P, 512], U8, name=f"w1_scales{b}{a}", align_bytes=64)
 
         def interleave(b, a):
+            view = grouped[b, a][:].rearrange("p (t m j) -> p m j t", t=4, j=4)
             for c0, c1, raw in raws[b, a]:
                 src = raw[:].rearrange("p j (m t) -> p m j t", t=4)
-                for e in (1, 0):
-                    copy = nc.scalar.copy if e == 1 and c0 == 0 else nc.vector.tensor_copy
-                    view = grouped[b, a, e][:].rearrange("p (t m j) -> p m j t", t=2, j=4)
-                    copy(view[:, c0 // 4 : c1 // 4], src[:, :, :, 2 * e : 2 * e + 2])
+                m0, n = c0 // 4, (c1 - c0) // 4
+                cut = {128: 76, 96: 48, 32: 32}[n]
+                if cut < n:
+                    nc.scalar.copy(view[:, m0 + cut : m0 + n], src[:, cut:n])
+                nc.vector.tensor_copy(view[:, m0 : m0 + cut], src[:, 0:cut])
 
         def quantise(b, a, step):
             for i in range(0, 2048, step):
                 o = slice(i // 4, (i + step) // 4)
-                e, r = divmod(i, 1024)
                 nc.vector.quantize_mx(
                     out=codes[b, a][:, o].bitcast(FP8),
                     scales=scales[b, a][:, o],
-                    in_=grouped[b, a, e][:, r : r + step],
+                    in_=grouped[b, a][:, i : i + step],
                 )
 
         def hidden_matmuls(b):
@@ -135,9 +135,8 @@ def tile_list_tabmlp_mix_res_kernel(
             return banks
 
         h_grouped, h_codes, h_scales = {}, {}, {}
-        shared = {(1, 0): "raw12_384", (1, 1): "grouped211"}
+        shared = {(1, 0): "raw12_384", (1, 1): "raw12_0"}
         for b in range(3):
-            h_codes[b] = keep.tile([P, S], U32, name=f"h_codes{b}", align_bytes=64)
             h_scales[b] = keep.tile([P, S], U8, name=f"h_scales{b}", align_bytes=64)
 
         def relu(engine, b, h, bank):
@@ -151,6 +150,7 @@ def tile_list_tabmlp_mix_res_kernel(
             h_grouped[b, h] = tile
 
         def hidden_quantise(b):
+            h_codes[b] = keep.tile([P, S], U32, name="grouped21" if b == 1 else f"h_codes{b}", align_bytes=64)
             for h in range(2):
                 toks = slice(HALF * h, HALF * (h + 1))
                 nc.vector.quantize_mx(
@@ -211,7 +211,7 @@ def tile_list_tabmlp_mix_res_kernel(
         interleave(2, 1)
         quantise(2, 1, 512)
         relu(nc.scalar, 1, 0, banks[0])
-        relu(nc.vector, 1, 1, banks[1])
+        relu(nc.scalar, 1, 1, banks[1])
         hidden_quantise(1)
         banks = hidden_matmuls(2)
         for m in range(2):

from contextlib import ExitStack

import concourse.mybir as mybir

FLOPS = 1207959552

P = 128
K, H, M, T, S = 1024, 1536, 512, 512, 256
HALF = 128
WORD_BYTES = 512 * T

F32 = mybir.dt.float32
BF16 = mybir.dt.bfloat16
I32 = mybir.dt.int32
U32 = mybir.dt.uint32
U16 = mybir.dt.uint16
U8 = mybir.dt.uint8
FP8 = mybir.dt.float8_e4m3fn_x4
FP4 = mybir.dt.float4_e2m1fn_x4
RELU = mybir.ActivationFunctionType.Relu


def tile_list_tabmlp_mix_res_kernel(
    tc, tab, w1, w8_words, w8_scales, w4_words, w4_scales, prev, offs, out
):
    nc = tc.nc
    with ExitStack() as ctx:
        keep = ctx.enter_context(tc.tile_pool(name="keep", bufs=1))
        psum = ctx.enter_context(tc.psum_pool(name="psum", bufs=1))

        offsets = keep.tile([P, S // 16], U16, name="offsets")
        table_words = [keep.tile([P, T], I32, name=f"table_words{a}", align_bytes=64) for a in range(2)]
        table_scales = keep.tile([P, T // 4], I32, name="table_scales", align_bytes=64)
        w2_scales = keep.tile([P, 3, M // 4], I32, name="w2_scales", align_bytes=64)
        w8_codes = keep.tile([P, M], I32, name="w8_codes", align_bytes=64)
        w4_codes = keep.tile([P, 2, M // 2], I32, name="w4_codes", align_bytes=64)
        prev_sb = keep.tile([P, 4, S], F32, name="prev_sb")

        nc.vector.memset(table_scales[:], 0)
        nc.vector.memset(w2_scales[:], 0)

        raws = {}

        def load_w1(a, b, c0, c1):
            raw = keep.tile([P, 4, c1 - c0], F32, name=f"raw{a}{b}_{c0}", align_bytes=64)
            rows = w1[512 * a : 512 * (a + 1), 512 * b + c0 : 512 * b + c1]
            nc.sync.dma_start(raw[:], rows.rearrange("(p j) c -> p j c", j=4))
            raws.setdefault((b, a), []).append((c0, c1, raw))

        tab_i32 = tab.bitcast(I32)
        tab_scale_rows = tab_i32[:, WORD_BYTES // 4 :].rearrange("a (q c) -> a q c", q=16)
        w8_rows = w8_scales.bitcast(I32)
        w4_rows = w4_scales.bitcast(I32)

        def load_w8_scales(q):
            nc.gpsimd.dma_start(w2_scales[32 * q : 32 * q + 4, 0, :], w8_rows[0, 4 * q : 4 * q + 4, :])

        def load_w4_scales(q):
            nc.gpsimd.dma_start(
                w2_scales[32 * q : 32 * q + 4, 1:3, :], w4_rows[:, 4 * q : 4 * q + 4, :].rearrange("a q c -> q a c")
            )

        for a in range(2):
            nc.sync.dma_start(
                table_words[a][:], tab_i32[a, 0 : WORD_BYTES // 4].rearrange("(p c) -> p c", p=P)
            )
        nc.sync.dma_start(offsets[:], offs)
        load_w1(0, 0, 0, 512)
        for q in range(4):
            nc.sync.dma_start(table_scales[32 * q : 32 * q + 8, :], tab_scale_rows[:, 4 * q : 4 * q + 4, :])
        for q in range(4):
            load_w8_scales(q)
        for q in range(4):
            load_w4_scales(q)
        load_w1(1, 0, 0, 512)
        load_w1(0, 1, 0, 512)
        load_w1(1, 1, 0, 512)
        load_w1(0, 2, 0, 512)
        load_w1(1, 2, 0, 384)
        load_w1(1, 2, 384, 512)
        nc.sync.dma_start(w8_codes[:], w8_words[0].rearrange("p n i -> p (n i)").bitcast(I32))
        nc.sync.dma_start(w4_codes[:], w4_words.bitcast(I32).rearrange("a p c -> p a c"))
        nc.sync.dma_start(prev_sb[:], prev.rearrange("(m p) j -> p m j", p=P))

        picked_words = []
        for a in range(2):
            words = keep.tile([P, S], U32, name=f"picked_words{a}", align_bytes=64)
            nc.vector.tensor_copy(words[:], table_words[a][:].bitcast(U32).indirect(offsets[:]))
            picked_words.append(words)
        picked_scales = keep.tile([P, S], U8, name="picked_scales", align_bytes=64)
        nc.vector.tensor_copy(picked_scales[:], table_scales[:].bitcast(U8).indirect(offsets[:]))

        grouped, codes, scales = {}, {}, {}
        for b in range(3):
            for a in range(2):
                grouped[b, a] = keep.tile([P, 2048], BF16, name=f"grouped{b}{a}", align_bytes=64)
                codes[b, a] = keep.tile([P, 512], U32, name=f"w1_codes{b}{a}", align_bytes=64)
                scales[b, a] = keep.tile([P, 512], U8, name=f"w1_scales{b}{a}", align_bytes=64)

        def interleave(b, a):
            view = grouped[b, a][:].rearrange("p (t m j) -> p m j t", t=4, j=4)
            for c0, c1, raw in raws[b, a]:
                src = raw[:].rearrange("p j (m t) -> p m j t", t=4)
                m0, n = c0 // 4, (c1 - c0) // 4
                cut = {128: 76, 96: 48, 32: 32}[n]
                if cut < n:
                    nc.scalar.copy(view[:, m0 + cut : m0 + n], src[:, cut:n])
                nc.vector.tensor_copy(view[:, m0 : m0 + cut], src[:, 0:cut])

        def quantise(b, a, step):
            for i in range(0, 2048, step):
                o = slice(i // 4, (i + step) // 4)
                nc.vector.quantize_mx(
                    out=codes[b, a][:, o].bitcast(FP8),
                    scales=scales[b, a][:, o],
                    in_=grouped[b, a][:, i : i + step],
                )

        def hidden_matmuls(b):
            banks = [psum.tile([P, 4, HALF], F32, name=f"hidden{b % 2}{h}") for h in range(2)]
            for t in range(4):
                cols = slice(HALF * t, HALF * (t + 1))
                for a in range(2):
                    for h in range(2):
                        toks = slice(HALF * h, HALF * (h + 1))
                        nc.tensor.matmul_mx(
                            out=banks[h][:, t, :],
                            lhsT=codes[b, a][:, cols].bitcast(FP8),
                            lhsT_scale=scales[b, a][:, cols],
                            rhs=picked_words[a][:, toks].bitcast(FP8),
                            rhs_scale=picked_scales[4 * a : P, toks],
                            start=a == 0,
                            stop=a == 1,
                        )
            return banks

        h_grouped, h_codes, h_scales = {}, {}, {}
        shared = {(1, 0): "raw12_384", (1, 1): "raw12_0"}
        for b in range(3):
            h_scales[b] = keep.tile([P, S], U8, name=f"h_scales{b}", align_bytes=64)

        def relu(engine, b, h, bank):
            name = shared.get((b, h), f"h_grouped{b}{h}")
            tile = keep.tile([P, HALF, 4], BF16, name=name, align_bytes=64)
            src = bank[:].rearrange("p t n -> p n t")
            if engine is nc.scalar:
                nc.scalar.activation(tile[:], src, RELU)
            else:
                nc.vector.tensor_scalar_max(tile[:], src, 0.0)
            h_grouped[b, h] = tile

        def hidden_quantise(b):
            h_codes[b] = keep.tile([P, S], U32, name="grouped21" if b == 1 else f"h_codes{b}", align_bytes=64)
            for h in range(2):
                toks = slice(HALF * h, HALF * (h + 1))
                nc.vector.quantize_mx(
                    out=h_codes[b][:, toks].bitcast(FP8),
                    scales=h_scales[b][:, toks],
                    in_=h_grouped[b, h][:].rearrange("p n t -> p (n t)"),
                )

        def out_matmul(acc, m, h, b):
            if b == 0:
                lhsT = w8_codes[:, HALF * m : HALF * (m + 1)].bitcast(FP8)
            else:
                lhsT = w4_codes[:, b - 1, 64 * m : 64 * (m + 1)].bitcast(FP4)
            nc.tensor.matmul_mx(
                out=acc[:],
                lhsT=lhsT,
                lhsT_scale=w2_scales[:, b, 32 * m : 32 * (m + 1)].bitcast(U8),
                rhs=h_codes[b][:, HALF * h : HALF * (h + 1)].bitcast(FP8),
                rhs_scale=h_scales[b][:, HALF * h : HALF * (h + 1)],
                start=b == 0,
                stop=b == 2,
            )

        acc = {}

        def start_out(m, h, name):
            acc[m, h] = psum.tile([P, HALF], F32, name=name)
            out_matmul(acc[m, h], m, h, 0)

        def finish_out(m):
            res = keep.tile([P, S], F32, name=f"res{m}")
            for h in range(2):
                out_matmul(acc[m, h], m, h, 2)
                toks = slice(HALF * h, HALF * (h + 1))
                nc.vector.tensor_add(res[:, toks], acc[m, h][:], prev_sb[:, m, toks])
                if m == 3:
                    queue = nc.scalar if h == 0 else nc.sync
                    queue.dma_start(out[P * m : P * (m + 1), toks], res[:, toks])
            if m < 3:
                queue = nc.scalar if m == 1 else nc.sync
                queue.dma_start(out[P * m : P * (m + 1), :], res[:])

        interleave(0, 0)
        quantise(0, 0, 1024)
        interleave(0, 1)
        quantise(0, 1, 1024)
        banks = hidden_matmuls(0)
        interleave(1, 0)
        quantise(1, 0, 1024)
        interleave(1, 1)
        relu(nc.scalar, 0, 0, banks[0])
        relu(nc.vector, 0, 1, banks[1])
        quantise(1, 1, 1024)
        banks = hidden_matmuls(1)
        hidden_quantise(0)
        interleave(2, 0)
        quantise(2, 0, 1024)
        interleave(2, 1)
        quantise(2, 1, 512)
        relu(nc.scalar, 1, 0, banks[0])
        relu(nc.scalar, 1, 1, banks[1])
        hidden_quantise(1)
        banks = hidden_matmuls(2)
        for m in range(2):
            for h in range(2):
                start_out(m, h, f"acc{m}{h}")
        for h in range(2):
            start_out(2, h, f"hidden1{h}")
        for m in range(3):
            for h in range(2):
                out_matmul(acc[m, h], m, h, 1)
        relu(nc.scalar, 2, 0, banks[0])
        relu(nc.vector, 2, 1, banks[1])
        for h in range(2):
            start_out(3, h, f"hidden0{h}")
            out_matmul(acc[3, h], 3, h, 1)
        hidden_quantise(2)
        for m in range(4):
            finish_out(m)
